import numpy as np
import ml_dtypes


def mxq(x, axis, fmt="e4m3"):
    dtype, down = {"e4m3": (ml_dtypes.float8_e4m3fn, 7), "e5m2": (ml_dtypes.float8_e5m2, 14)}[fmt]
    v = np.moveaxis(np.asarray(x, np.float32).astype(ml_dtypes.bfloat16).astype(np.float64), axis, -1)
    blocks = v.reshape(v.shape[:-1] + (-1, 32))
    amax = np.abs(blocks).max(-1, keepdims=True)
    byte = np.maximum(np.where(amax > 0, np.frexp(amax)[1] - 1 + 127, 0) - down, 1)
    scale = np.exp2(byte - 127.0)
    codes = (blocks / scale).astype(np.float32).astype(dtype).astype(np.float64)
    return np.moveaxis((codes * scale).reshape(v.shape), -1, axis)


WIDE = False


def mx_kscale(k):
    if not WIDE:
        return np.ones(k)
    levels = np.array([10, -10, 5, -5, 0])
    if k % 512:
        return np.exp2(np.random.permutation(np.resize(levels, k // 32))).repeat(32)
    a = np.empty((k // 512, 16))
    for p in range(k // 512):
        a[p, :8] = np.random.permutation(np.resize(levels, 8))
        for g in range(8):
            far = levels[np.abs(levels - a[p, g]) >= 10]
            a[p, g + 8] = far[np.random.randint(len(far))]
    return np.exp2(a.ravel()).repeat(32)


def f64(x):
    return np.asarray(x).astype(np.float64)


def striped(idx):
    return np.tile(np.asarray(idx).reshape(-1, 16).T, (8, 1)).astype(np.uint16)


def unstriped(offs):
    return offs[:16].T.reshape(-1).astype(np.int64)


E2M1 = np.array([0.0, 0.5, 1.0, 1.5, 2.0, 3.0, 4.0, 6.0, -0.0, -0.5, -1.0, -1.5, -2.0, -3.0, -4.0, -6.0])


def pack_weight(w, fmt):
    k, n = w.shape
    w = f64(np.asarray(w, np.float32).astype(ml_dtypes.bfloat16)).reshape(k // 32, 32, n)
    amax = np.abs(w).max(1)
    if fmt == "e4m3":
        byte = np.frexp(amax)[1] - 1 + 127 - 7
    else:
        mant, ex = np.frexp(amax / 6.0)
        byte = np.where(mant > 0.5, ex, ex - 1) + 127
    byte = np.clip(np.where(amax > 0, byte, 1), 1, 254)
    scaled = (w * np.exp2(127.0 - byte)[:, None, :]).reshape(k, n).astype(np.float32)
    by_word = np.ascontiguousarray(scaled.reshape(k // 512, 128, 4, n).transpose(0, 1, 3, 2))
    if fmt == "e4m3":
        words = by_word.astype(ml_dtypes.float8_e4m3fn).view(np.uint8)
    else:
        c = by_word.astype(ml_dtypes.float4_e2m1fn).view(np.uint8) & 0xF
        words = (c[..., 0::2] | (c[..., 1::2] << 4)).reshape(k // 512, 128, 2 * n)
    return np.ascontiguousarray(words), np.ascontiguousarray(byte.astype(np.uint8).reshape(k // 512, 16, n))


def unpack_weight(words, scales, fmt):
    g, _, n = scales.shape
    words = np.ascontiguousarray(words).reshape(g, 128, n, -1)
    if fmt == "e4m3":
        vals = words.view(ml_dtypes.float8_e4m3fn).astype(np.float64)
    else:
        nib = np.empty((g, 128, n, 4), np.uint8)
        nib[..., 0::2] = words & 0xF
        nib[..., 1::2] = words >> 4
        vals = E2M1[nib]
    vals = vals * np.repeat(np.exp2(scales.astype(np.float64) - 127.0), 8, axis=1)[..., None]
    return vals.transpose(0, 1, 3, 2).reshape(g * 512, n)


def bf(x):
    return np.asarray(x, np.float32).astype(ml_dtypes.bfloat16)


def planes(Y):
    r, m = Y.shape
    b = f64(bf(Y)).reshape(r // 32, 32, m)
    amax = np.abs(b).max(1)
    byte = np.clip(np.where(amax > 0, np.frexp(amax)[1] - 1 + 127 - 7, 1), 1, 254)
    codes = (b * np.exp2(127.0 - byte)[:, None, :]).reshape(r, m).astype(np.float32).astype(ml_dtypes.float8_e4m3fn).view(np.uint8)
    words = codes.reshape(r // 512, 128, 4, m).transpose(0, 1, 3, 2)
    return np.ascontiguousarray(words), np.ascontiguousarray(byte.astype(np.uint8).reshape(r // 512, 16, m))


K, T, J, N = 512, 1024, 512, 512


def setup_inputs():
    n = np.random.standard_normal
    idx = np.random.permutation(T)[:J]
    idx2 = np.random.permutation(T)[:J]
    fk = mx_kscale(K)
    wap = pack_weight(n((K, N)) * 1 / np.sqrt(K) * fk[:, None], "e4m3")
    return {
        "xf": (n((K, T)) / fk[:, None]).astype(np.float32),
        "wa_words": wap[0],
        "wa_scales": wap[1],
        "ga": (np.random.uniform(0.4, 1.2, (1, J))).astype(np.float32),
        "old": (1.0 * n((N, T))).astype(np.float32),
        "offs": striped(idx),
        "offs2": striped(idx2),
    }


def reference(xf, wa_words, wa_scales, ga, old, offs, offs2):
    idx = unstriped(offs)
    idx2 = unstriped(offs2)
    wau = unpack_weight(wa_words, wa_scales, "e4m3")
    d = f64(xf)[:, idx] - f64(xf)[:, idx2]
    dq = mxq(d, 0, "e4m3")
    p = wau.T @ dq
    pw = p * f64(ga)
    pp = np.zeros((N, T))
    pp[:, idx2] = pw
    y = 0.5 * f64(old) - pp
    words, scales = planes(y)
    return y, words, scales

@@ -1,0 +1,217 @@
+from contextlib import ExitStack
+
+import concourse.mybir as mybir
+from concourse.masks import make_identity
+
+K, T, J, N = 512, 1024, 512, 512
+FLOPS = 2 * K * J * N
+
+F32 = mybir.dt.float32
+BF16 = mybir.dt.bfloat16
+I32 = mybir.dt.int32
+U32 = mybir.dt.uint32
+U16 = mybir.dt.uint16
+U8 = mybir.dt.uint8
+FP8X4 = mybir.dt.float8_e4m3fn_x4
+ALU = mybir.AluOpType
+COPY = mybir.ActivationFunctionType.Copy
+
+P = 128
+PACK = 4
+HALF = J // 2
+LIST_COLS = J // 16
+CHUNK = 256
+
+
+def tile_moe_expert_on_gap_writes_to_partner_pl_kernel(
+    tc, xf, wa_words, wa_scales, ga, old, offs, offs2, out_0, out_1, out_2
+):
+    nc = tc.nc
+    with ExitStack() as ctx:
+        keep = ctx.enter_context(tc.tile_pool(name="keep", bufs=1))
+        psum = ctx.enter_context(tc.psum_pool(name="psum", bufs=1))
+
+        xf_rows = xf.rearrange("(p r) t -> p r t", r=PACK)
+        old_rows = old.rearrange("(p r) t -> p r t", r=PACK)
+        out_rows = out_0.rearrange("(p r) t -> p r t", r=PACK)
+
+        own_list = keep.tile([P, LIST_COLS], U16, name="own_list")
+        partner_list = keep.tile([P, LIST_COLS], U16, name="partner_list")
+        x = [keep.tile([P, T], F32, name=f"x{r}") for r in range(PACK)]
+        old_sb = [keep.tile([P, T], F32, name=f"old{r}") for r in range(PACK)]
+        placed = [keep.tile([P, T], F32, name=f"placed{r}") for r in range(PACK)]
+        w_codes = keep.tile([P, N], U32, name="w_codes", align_bytes=64)
+        w_scales = keep.tile([P, N], U8, name="w_scales", align_bytes=64)
+        gate = keep.tile([P, J // P], F32, name="gate")
+        ident = keep.tile([P, P], F32, name="ident")
+
+        nc.vector.memset(w_scales[:].bitcast(I32), 0)
+        nc.sync.dma_start(out=x[0][:], in_=xf_rows[:, 0, :])
+        nc.sync.dma_start(partner_list[:], offs2)
+        nc.sync.dma_start(own_list[:], offs)
+        for r in range(1, PACK):
+            nc.sync.dma_start(out=x[r][:], in_=xf_rows[:, r, :])
+        nc.sync.dma_start(
+            out=w_codes[:].bitcast(I32),
+            in_=wa_words[0].rearrange("p n r -> p (n r)").bitcast(I32),
+        )
+        for q in range(4):
+            nc.sync.dma_start(
+                out=w_scales[32 * q : 32 * q + 4, :].bitcast(I32),
+                in_=wa_scales[0, 4 * q : 4 * q + 4, :].bitcast(I32),
+            )
+        with nc.allow_non_contiguous_dma(reason="one gate value a partition"):
+            nc.sync.dma_start(out=gate[:], in_=ga[0].rearrange("(b p) -> p b", p=P))
+        for r in range(PACK):
+            nc.sync.dma_start(out=old_sb[r][:], in_=old_rows[:, r, :])
+
+        for r in range(2):
+            nc.vector.memset(placed[r][:].bitcast(I32), 0)
+        make_identity(nc, ident[:])
+        for r in range(2, PACK):
+            nc.gpsimd.memset(placed[r][:], 0.0)
+
+        d_codes = keep.tile([P, J], U32, name="d_codes", align_bytes=64)
+        d_scales = keep.tile([P, J], U8, name="d_scales", align_bytes=64)
+
+        def list_half(lst, h):
+            return lst[:, h * LIST_COLS // 2 : (h + 1) * LIST_COLS // 2]
+
+        def gather_partner(dst, r, h):
+            nc.vector.tensor_copy(dst, x[r][:].indirect(list_half(partner_list, h)))
+
+        def gather_gap(dst, partner, r, h):
+            nc.vector.tensor_tensor(dst, x[r][:].indirect(list_half(own_list, h)), partner, ALU.subtract)
+
+        def interleave(gap, h):
+            grouped = keep.tile([P, HALF, PACK], BF16, name=f"grouped{h}", tag=f"grouped{h}", align_bytes=64)
+            nc.scalar.activation(
+                out=grouped[:].rearrange("p (c i) r -> p c r i", i=4),
+                in_=gap[:].rearrange("p r (c i) -> p c r i", i=4),
+                func=COPY,
+            )
+            return grouped
+
+        def quantise(grouped, h):
+            cols = slice(h * HALF, (h + 1) * HALF)
+            nc.vector.quantize_mx(
+                out=d_codes[:, cols].bitcast(FP8X4),
+                scales=d_scales[:, cols],
+                in_=grouped[:].rearrange("p c r -> p (c r)"),
+            )
+
+        def multiply(h):
+            banks = [psum.tile([P, HALF], F32, name=f"turned{h}{r}", tag=f"turned{r}") for r in range(PACK)]
+            for b in range(2 * h, 2 * h + 2):
+                cols = slice(b * P, (b + 1) * P)
+                acc = psum.tile([P, N], F32, name=f"acc{b}")
+                nc.tensor.matmul_mx(
+                    out=acc[:],
+                    lhsT=d_codes[:, cols].bitcast(FP8X4),
+                    lhsT_scale=d_scales[:, cols],
+                    rhs=w_codes[:].bitcast(FP8X4),
+                    rhs_scale=w_scales[:],
+                    start=True,
+                    stop=True,
+                )
+                gated = keep.tile([P, PACK, P], F32, name=f"gated{b}", tag=f"gated{b}")
+                nc.scalar.activation(
+                    out=gated[:],
+                    in_=acc[:].rearrange("p (m r) -> p r m", r=PACK),
+                    func=COPY,
+                    scale=gate[:, b : b + 1],
+                )
+                for r in range(PACK):
+                    nc.tensor.transpose(banks[r][:, (b % 2) * P : (b % 2 + 1) * P], gated[:, r, :], ident[:])
+            return banks
+
+        def scatter(r, lst, values):
+            nc.vector.tensor_copy(placed[r][:].indirect(lst), values)
+
+        gap0 = keep.tile([P, PACK, HALF], F32, name="gap0", tag="gap0")
+        for r in range(PACK):
+            partner = keep.tile([P, HALF], F32, name=f"partner{r}", tag=f"partner{r}")
+            gather_partner(partner[:], r, 0)
+            gather_gap(gap0[:, r, :], partner[:], r, 0)
+        grouped0 = interleave(gap0, 0)
+        early = keep.tile([P, 2, HALF], F32, name="early", tag="partner3")
+        for r in range(2):
+            gather_partner(early[:, r, :], r, 1)
+        quantise(grouped0, 0)
+        banks0 = multiply(0)
+        pw_first = keep.tile([P, HALF], F32, name="pw_first")
+        nc.scalar.copy(out=pw_first[:], in_=banks0[0][:])
+        late = keep.tile([P, 2, HALF], F32, name="late", tag="gap0")
+        gap1 = keep.tile([P, PACK, HALF], F32, name="gap1", tag="grouped0", align_bytes=64)
+        for r in range(2):
+            gather_partner(late[:, r, :], 2 + r, 1)
+        for r in range(PACK):
+            gather_gap(gap1[:, r, :], early[:, r, :] if r < 2 else late[:, r - 2, :], r, 1)
+        grouped1 = interleave(gap1, 1)
+        scatter(0, list_half(partner_list, 0), pw_first[:])
+        quantise(grouped1, 1)
+        pw0 = keep.tile([P, 2, HALF], F32, name="pw0", tag="grouped0", align_bytes=64)
+        pw_last = keep.tile([P, J], F32, name="pw_last", tag="gap0")
+        for r in range(1, 3):
+            nc.scalar.copy(out=pw0[:, r - 1, :], in_=banks0[r][:])
+        nc.scalar.copy(out=pw_last[:, :HALF], in_=banks0[3][:])
+        for r in range(1, 3):
+            scatter(r, list_half(partner_list, 0), pw0[:, r - 1, :])
+        banks1 = multiply(1)
+        pw1 = keep.tile([P, 3, HALF], F32, name="pw1")
+        for r in range(3):
+            nc.scalar.copy(out=pw1[:, r, :], in_=banks1[r][:])
+        nc.scalar.copy(out=pw_last[:, HALF:], in_=banks1[3][:])
+
+        halved = keep.tile([P, 3, T], F32, name="halved", tag="gated3")
+        y = keep.tile([P, PACK, T], F32, name="y")
+        y_grouped = keep.tile([P, T, PACK], BF16, name="y_grouped", align_bytes=64)
+        y_codes = keep.tile([P, T], U32, name="y_codes", align_bytes=64)
+        y_scales = keep.tile([P, T], U8, name="y_scales", align_bytes=64)
+        for r in range(3):
+            nc.scalar.activation(out=halved[:, r, :], in_=old_sb[r][:], func=COPY, scale=0.5)
+
+        def pair_views(first, cols):
+            dst = y_grouped[:, cols, first : first + 2].rearrange("p (c i) r -> p c r i", i=2)
+            src = y[:, first : first + 2, cols].rearrange("p r (c i) -> p c r i", i=2)
+            return dst, src
+
+        for r in range(3):
+            scatter(r, list_half(partner_list, 1), pw1[:, r, :])
+            for c in range(2):
+                cols = slice(c * T // 2, (c + 1) * T // 2)
+                nc.gpsimd.tensor_tensor(y[:, r, cols], halved[:, r, cols], placed[r][:, cols], ALU.subtract)
+                if r == 1:
+                    dst, src = pair_views(0, cols)
+                    nc.scalar.copy(out=dst, in_=src)
+            nc.sync.dma_start(out=out_rows[:, r, :], in_=y[:, r, :])
+        scatter(3, partner_list[:], pw_last[:])
+
+        chunks = [slice(c * CHUNK, (c + 1) * CHUNK) for c in range(T // CHUNK)]
+        for c, cols in enumerate(chunks):
+            nc.vector.scalar_tensor_tensor(
+                y[:, 3, cols], old_sb[3][:, cols], 0.5, placed[3][:, cols], ALU.mult, ALU.subtract
+            )
+            if c % 2 == 1:
+                both = slice((c - 1) * CHUNK, (c + 1) * CHUNK)
+                nc.sync.dma_start(out=out_rows[:, 3, both], in_=y[:, 3, both])
+        for c, cols in enumerate(chunks):
+            dst, src = pair_views(2, cols)
+            if c in (0, 3):
+                nc.scalar.copy(out=dst, in_=src)
+            else:
+                nc.vector.tensor_copy(out=dst, in_=src)
+        words_out = out_1[0].rearrange("p c r -> p (c r)").bitcast(I32)
+        for c, cols in enumerate(chunks):
+            nc.vector.quantize_mx(
+                out=y_codes[:, cols].bitcast(FP8X4),
+                scales=y_scales[:, cols],
+                in_=y_grouped[:, cols, :].rearrange("p c r -> p (c r)"),
+            )
+            nc.sync.dma_start(out=words_out[:, cols], in_=y_codes[:, cols].bitcast(I32))
+        for q in range(4):
+            eng = nc.sync if q % 2 == 0 else nc.scalar
+            eng.dma_start(
+                out=out_2[0, 4 * q : 4 * q + 4, :].bitcast(I32),
+                in_=y_scales[32 * q : 32 * q + 4, :].bitcast(I32),
+            )

@@ -71,146 +71,167 @@ def tile_moe_expert_on_gap_writes_to_partner_pl_kernel(
         for r in range(2, PACK):
             nc.gpsimd.memset(placed[r][:], 0.0)
 
-        d_codes = keep.tile([P, J], U32, name="d_codes", align_bytes=64)
-        d_scales = keep.tile([P, J], U8, name="d_scales", align_bytes=64)
+        def entries(lst, a, b):
+            return lst[:, a // 16 : b // 16]
 
-        def list_half(lst, h):
-            return lst[:, h * LIST_COLS // 2 : (h + 1) * LIST_COLS // 2]
+        def gather_pair(dst, r, h):
+            nc.vector.tensor_copy(dst[:, 0, :], x[r][:].indirect(entries(own_list, h * HALF, (h + 1) * HALF)))
+            nc.vector.tensor_copy(dst[:, 1, :], x[r][:].indirect(entries(partner_list, h * HALF, (h + 1) * HALF)))
 
-        def gather_partner(dst, r, h):
-            nc.vector.tensor_copy(dst, x[r][:].indirect(list_half(partner_list, h)))
+        def subtract(grouped, pair, r):
+            nc.gpsimd.tensor_tensor(grouped[:, :, r], pair[:, 0, :], pair[:, 1, :], ALU.subtract)
 
-        def gather_gap(dst, partner, r, h):
-            nc.vector.tensor_tensor(dst, x[r][:].indirect(list_half(own_list, h)), partner, ALU.subtract)
-
-        def interleave(gap, h):
-            grouped = keep.tile([P, HALF, PACK], BF16, name=f"grouped{h}", tag=f"grouped{h}", align_bytes=64)
-            nc.scalar.activation(
-                out=grouped[:].rearrange("p (c i) r -> p c r i", i=4),
-                in_=gap[:].rearrange("p r (c i) -> p c r i", i=4),
-                func=COPY,
-            )
-            return grouped
-
-        def quantise(grouped, h):
-            cols = slice(h * HALF, (h + 1) * HALF)
+        def quantise(grouped, h, tag):
+            codes = keep.tile([P, HALF], U32, name=f"d_codes{h}", tag=tag, align_bytes=64)
+            scales = keep.tile([P, HALF], U8, name=f"d_scales{h}", align_bytes=64)
             nc.vector.quantize_mx(
-                out=d_codes[:, cols].bitcast(FP8X4),
-                scales=d_scales[:, cols],
-                in_=grouped[:].rearrange("p c r -> p (c r)"),
+                out=codes[:].bitcast(FP8X4), scales=scales[:], in_=grouped[:].rearrange("p c r -> p (c r)")
             )
+            return codes, scales
 
-        def multiply(h):
+        def multiply(codes, scales, h, urgent):
             banks = [psum.tile([P, HALF], F32, name=f"turned{h}{r}", tag=f"turned{r}") for r in range(PACK)]
-            for b in range(2 * h, 2 * h + 2):
+            sums = []
+            for b in range(2):
                 cols = slice(b * P, (b + 1) * P)
-                acc = psum.tile([P, N], F32, name=f"acc{b}")
+                acc = psum.tile([P, N], F32, name=f"acc{h}{b}")
                 nc.tensor.matmul_mx(
                     out=acc[:],
-                    lhsT=d_codes[:, cols].bitcast(FP8X4),
-                    lhsT_scale=d_scales[:, cols],
+                    lhsT=codes[:, cols].bitcast(FP8X4),
+                    lhsT_scale=scales[:, cols],
                     rhs=w_codes[:].bitcast(FP8X4),
                     rhs_scale=w_scales[:],
                     start=True,
                     stop=True,
                 )
-                gated = keep.tile([P, PACK, P], F32, name=f"gated{b}", tag=f"gated{b}")
-                nc.scalar.activation(
-                    out=gated[:],
-                    in_=acc[:].rearrange("p (m r) -> p r m", r=PACK),
-                    func=COPY,
-                    scale=gate[:, b : b + 1],
-                )
-                for r in range(PACK):
-                    nc.tensor.transpose(banks[r][:, (b % 2) * P : (b % 2 + 1) * P], gated[:, r, :], ident[:])
+                sums.append(acc[:].rearrange("p (m r) -> p r m", r=PACK))
+            for first, last in ((0, 1), (1, PACK)):
+                for b in range(2):
+                    gated = keep.tile(
+                        [P, last - first, P], F32, name=f"gated{h}{b}{first}", tag=f"gated{h}{b}{first}"
+                    )
+                    nc.scalar.activation(
+                        out=gated[:],
+                        in_=sums[b][:, first:last, :],
+                        func=COPY,
+                        scale=gate[:, 2 * h + b : 2 * h + b + 1],
+                    )
+                    for r in range(first, last):
+                        nc.tensor.transpose(banks[r][:, b * P : (b + 1) * P], gated[:, r - first, :], ident[:])
+                if first == 0:
+                    nc.scalar.copy(out=urgent, in_=banks[0][:, : urgent.shape[1]])
             return banks
 
-        def scatter(r, lst, values):
-            nc.vector.tensor_copy(placed[r][:].indirect(lst), values)
+        def scatter(r, a, b, values):
+            nc.vector.tensor_copy(placed[r][:].indirect(entries(partner_list, a, b)), values)
 
-        gap0 = keep.tile([P, PACK, HALF], F32, name="gap0", tag="gap0")
+        grouped0 = keep.tile([P, HALF, PACK], BF16, name="grouped0", tag="grouped", align_bytes=64)
         for r in range(PACK):
-            partner = keep.tile([P, HALF], F32, name=f"partner{r}", tag=f"partner{r}")
-            gather_partner(partner[:], r, 0)
-            gather_gap(gap0[:, r, :], partner[:], r, 0)
-        grouped0 = interleave(gap0, 0)
-        early = keep.tile([P, 2, HALF], F32, name="early", tag="partner3")
-        for r in range(2):
-            gather_partner(early[:, r, :], r, 1)
-        quantise(grouped0, 0)
-        banks0 = multiply(0)
-        pw_first = keep.tile([P, HALF], F32, name="pw_first")
-        nc.scalar.copy(out=pw_first[:], in_=banks0[0][:])
-        late = keep.tile([P, 2, HALF], F32, name="late", tag="gap0")
-        gap1 = keep.tile([P, PACK, HALF], F32, name="gap1", tag="grouped0", align_bytes=64)
-        for r in range(2):
-            gather_partner(late[:, r, :], 2 + r, 1)
-        for r in range(PACK):
-            gather_gap(gap1[:, r, :], early[:, r, :] if r < 2 else late[:, r - 2, :], r, 1)
-        grouped1 = interleave(gap1, 1)
-        scatter(0, list_half(partner_list, 0), pw_first[:])
-        quantise(grouped1, 1)
-        pw0 = keep.tile([P, 2, HALF], F32, name="pw0", tag="grouped0", align_bytes=64)
-        pw_last = keep.tile([P, J], F32, name="pw_last", tag="gap0")
-        for r in range(1, 3):
-            nc.scalar.copy(out=pw0[:, r - 1, :], in_=banks0[r][:])
-        nc.scalar.copy(out=pw_last[:, :HALF], in_=banks0[3][:])
-        for r in range(1, 3):
-            scatter(r, list_half(partner_list, 0), pw0[:, r - 1, :])
-        banks1 = multiply(1)
-        pw1 = keep.tile([P, 3, HALF], F32, name="pw1")
-        for r in range(3):
-            nc.scalar.copy(out=pw1[:, r, :], in_=banks1[r][:])
-        nc.scalar.copy(out=pw_last[:, HALF:], in_=banks1[3][:])
+            pair = keep.tile([P, 2, HALF], F32, name=f"pair0{r}", tag=f"pair0{r}")
+            gather_pair(pair, r, 0)
+            subtract(grouped0, pair, r)
+        pair13 = keep.tile([P, 2, HALF], F32, name="pair13")
+        gather_pair(pair13, 3, 1)
+        codes0, scales0 = quantise(grouped0, 0, "d_codes0")
+        halved0 = keep.tile([P, T], F32, name="halved0")
+        nc.scalar.activation(out=halved0[:], in_=old_sb[0][:], func=COPY, scale=0.5)
+        pw_first = keep.tile([P, P], F32, name="pw_first", tag="pw_first", align_bytes=64)
+        banks0 = multiply(codes0, scales0, 0, pw_first[:])
+        pw_late = keep.tile([P, 2, J], F32, name="pw_late")
+        for r in range(2, PACK):
+            nc.scalar.copy(out=pw_late[:, r - 2, :HALF], in_=banks0[r][:])
 
-        halved = keep.tile([P, 3, T], F32, name="halved", tag="gated3")
-        y = keep.tile([P, PACK, T], F32, name="y")
+        grouped1 = keep.tile([P, HALF, PACK], BF16, name="grouped1", tag="grouped", align_bytes=64)
+        subtract(grouped1, pair13, 3)
+        pairs1 = keep.tile([P, 3, 2, HALF], F32, name="pairs1", tag="pair03")
+        for r in (2, 1, 0):
+            gather_pair(pairs1[:, r, :, :], r, 1)
+            subtract(grouped1, pairs1[:, r, :, :], r)
+        scatter(0, 0, P, pw_first[:])
+        codes1, scales1 = quantise(grouped1, 1, "pw_first")
+        pw_next = keep.tile([P, P + HALF], F32, name="pw_next", tag="pair03")
+        nc.scalar.copy(out=pw_next[:, :P], in_=banks0[0][:, P:])
+        nc.scalar.copy(out=pw_next[:, P:], in_=banks0[1][:])
+        scatter(0, P, HALF, pw_next[:, :P])
+        scatter(1, 0, HALF, pw_next[:, P:])
+
+        pw1 = keep.tile([P, 2, HALF], F32, name="pw1")
+        banks1 = multiply(codes1, scales1, 1, pw1[:, 0, :])
+        nc.scalar.copy(out=pw1[:, 1, :], in_=banks1[1][:])
+        for r in range(2, PACK):
+            nc.scalar.copy(out=pw_late[:, r - 2, HALF:], in_=banks1[r][:])
+
+        halved1 = keep.tile([P, T], F32, name="halved1", tag="gated101")
+        y = keep.tile([P, PACK, T], F32, name="y", tag="gated111")
+        halved = [halved0[:], halved1[:], y[:, 3, :]]
+        for r in range(1, 3):
+            nc.scalar.activation(out=halved[r], in_=old_sb[r][:], func=COPY, scale=0.5)
         y_grouped = keep.tile([P, T, PACK], BF16, name="y_grouped", align_bytes=64)
         y_codes = keep.tile([P, T], U32, name="y_codes", align_bytes=64)
         y_scales = keep.tile([P, T], U8, name="y_scales", align_bytes=64)
-        for r in range(3):
-            nc.scalar.activation(out=halved[:, r, :], in_=old_sb[r][:], func=COPY, scale=0.5)
 
         def pair_views(first, cols):
             dst = y_grouped[:, cols, first : first + 2].rearrange("p (c i) r -> p c r i", i=2)
             src = y[:, first : first + 2, cols].rearrange("p r (c i) -> p c r i", i=2)
             return dst, src
 
-        for r in range(3):
-            scatter(r, list_half(partner_list, 1), pw1[:, r, :])
-            for c in range(2):
-                cols = slice(c * T // 2, (c + 1) * T // 2)
-                nc.gpsimd.tensor_tensor(y[:, r, cols], halved[:, r, cols], placed[r][:, cols], ALU.subtract)
-                if r == 1:
-                    dst, src = pair_views(0, cols)
-                    nc.scalar.copy(out=dst, in_=src)
-            nc.sync.dma_start(out=out_rows[:, r, :], in_=y[:, r, :])
-        scatter(3, partner_list[:], pw_last[:])
+        def combine_gpsimd(r, cols):
+            nc.gpsimd.tensor_tensor(y[:, r, cols], halved[r][:, cols], placed[r][:, cols], ALU.subtract)
 
-        chunks = [slice(c * CHUNK, (c + 1) * CHUNK) for c in range(T // CHUNK)]
-        for c, cols in enumerate(chunks):
+        def combine_vector(r, cols):
             nc.vector.scalar_tensor_tensor(
-                y[:, 3, cols], old_sb[3][:, cols], 0.5, placed[3][:, cols], ALU.mult, ALU.subtract
+                y[:, r, cols], old_sb[r][:, cols], 0.5, placed[r][:, cols], ALU.mult, ALU.subtract
             )
-            if c % 2 == 1:
-                both = slice((c - 1) * CHUNK, (c + 1) * CHUNK)
-                nc.sync.dma_start(out=out_rows[:, 3, both], in_=y[:, 3, both])
-        for c, cols in enumerate(chunks):
-            dst, src = pair_views(2, cols)
-            if c in (0, 3):
-                nc.scalar.copy(out=dst, in_=src)
-            else:
-                nc.vector.tensor_copy(out=dst, in_=src)
+
+        left, right = slice(0, T // 2), slice(T // 2, T)
+        chunks = [slice(c * CHUNK, (c + 1) * CHUNK) for c in range(T // CHUNK)]
+
+        scatter(0, HALF, J, pw1[:, 0, :])
+        combine_gpsimd(0, slice(0, T))
+        nc.sync.dma_start(out=out_rows[:, 0, :], in_=y[:, 0, :])
+        scatter(1, HALF, J, pw1[:, 1, :])
+        for cols in (left, right):
+            combine_gpsimd(1, cols)
+            dst, src = pair_views(0, cols)
+            nc.scalar.copy(out=dst, in_=src)
+        nc.sync.dma_start(out=out_rows[:, 1, :], in_=y[:, 1, :])
+        scatter(2, 0, J, pw_late[:, 0, :])
+        for cols in (left, right):
+            combine_gpsimd(2, cols)
+            nc.sync.dma_start(out=out_rows[:, 2, cols], in_=y[:, 2, cols])
+        scatter(3, 0, J, pw_late[:, 1, :])
+
+        combine_vector(3, chunks[0])
+        combine_vector(3, chunks[1])
+        nc.sync.dma_start(out=out_rows[:, 3, left], in_=y[:, 3, left])
+        combine_vector(3, chunks[2])
+        combine_vector(3, chunks[3])
+        nc.sync.dma_start(out=out_rows[:, 3, right], in_=y[:, 3, right])
+
         words_out = out_1[0].rearrange("p c r -> p (c r)").bitcast(I32)
-        for c, cols in enumerate(chunks):
+
+        def quantise_y(cols):
             nc.vector.quantize_mx(
                 out=y_codes[:, cols].bitcast(FP8X4),
                 scales=y_scales[:, cols],
                 in_=y_grouped[:, cols, :].rearrange("p c r -> p (c r)"),
             )
+
+        def store_words(cols):
             nc.sync.dma_start(out=words_out[:, cols], in_=y_codes[:, cols].bitcast(I32))
+
+        for cols in (chunks[0], chunks[1], slice(T - P, T)):
+            dst, src = pair_views(2, cols)
+            nc.scalar.copy(out=dst, in_=src)
+        dst, src = pair_views(2, slice(T // 2, T - P))
+        nc.vector.tensor_copy(out=dst, in_=src)
+        quantise_y(chunks[0])
+        quantise_y(chunks[1])
+        store_words(left)
+        quantise_y(right)
+        store_words(right)
         for q in range(4):
-            eng = nc.sync if q % 2 == 0 else nc.scalar
+            eng = nc.scalar if q % 2 == 0 else nc.sync
             eng.dma_start(
                 out=out_2[0, 4 * q : 4 * q + 4, :].bitcast(I32),
                 in_=y_scales[32 * q : 32 * q + 4, :].bitcast(I32),

from contextlib import ExitStack

import concourse.mybir as mybir
from concourse.masks import make_identity

K, T, J, N = 512, 1024, 512, 512
FLOPS = 2 * K * J * N

F32 = mybir.dt.float32
BF16 = mybir.dt.bfloat16
I32 = mybir.dt.int32
U32 = mybir.dt.uint32
U16 = mybir.dt.uint16
U8 = mybir.dt.uint8
FP8X4 = mybir.dt.float8_e4m3fn_x4
ALU = mybir.AluOpType
COPY = mybir.ActivationFunctionType.Copy

P = 128
PACK = 4
HALF = J // 2
LIST_COLS = J // 16
CHUNK = 256


def tile_moe_expert_on_gap_writes_to_partner_pl_kernel(
    tc, xf, wa_words, wa_scales, ga, old, offs, offs2, out_0, out_1, out_2
):
    nc = tc.nc
    with ExitStack() as ctx:
        keep = ctx.enter_context(tc.tile_pool(name="keep", bufs=1))
        psum = ctx.enter_context(tc.psum_pool(name="psum", bufs=1))

        xf_rows = xf.rearrange("(p r) t -> p r t", r=PACK)
        old_rows = old.rearrange("(p r) t -> p r t", r=PACK)
        out_rows = out_0.rearrange("(p r) t -> p r t", r=PACK)

        own_list = keep.tile([P, LIST_COLS], U16, name="own_list")
        partner_list = keep.tile([P, LIST_COLS], U16, name="partner_list")
        x = [keep.tile([P, T], F32, name=f"x{r}") for r in range(PACK)]
        old_sb = [keep.tile([P, T], F32, name=f"old{r}") for r in range(PACK)]
        placed = [keep.tile([P, T], F32, name=f"placed{r}") for r in range(PACK)]
        w_codes = keep.tile([P, N], U32, name="w_codes", align_bytes=64)
        w_scales = keep.tile([P, N], U8, name="w_scales", align_bytes=64)
        gate = keep.tile([P, J // P], F32, name="gate")
        ident = keep.tile([P, P], F32, name="ident")

        nc.vector.memset(w_scales[:].bitcast(I32), 0)
        nc.sync.dma_start(out=x[0][:], in_=xf_rows[:, 0, :])
        nc.sync.dma_start(partner_list[:], offs2)
        nc.sync.dma_start(own_list[:], offs)
        for r in range(1, PACK):
            nc.sync.dma_start(out=x[r][:], in_=xf_rows[:, r, :])
        nc.sync.dma_start(
            out=w_codes[:].bitcast(I32),
            in_=wa_words[0].rearrange("p n r -> p (n r)").bitcast(I32),
        )
        for q in range(4):
            nc.sync.dma_start(
                out=w_scales[32 * q : 32 * q + 4, :].bitcast(I32),
                in_=wa_scales[0, 4 * q : 4 * q + 4, :].bitcast(I32),
            )
        with nc.allow_non_contiguous_dma(reason="one gate value a partition"):
            nc.sync.dma_start(out=gate[:], in_=ga[0].rearrange("(b p) -> p b", p=P))
        for r in range(PACK):
            nc.sync.dma_start(out=old_sb[r][:], in_=old_rows[:, r, :])

        for r in range(2):
            nc.vector.memset(placed[r][:].bitcast(I32), 0)
        make_identity(nc, ident[:])
        for r in range(2, PACK):
            nc.gpsimd.memset(placed[r][:], 0.0)

        def entries(lst, a, b):
            return lst[:, a // 16 : b // 16]

        def gather_pair(dst, r, h):
            nc.vector.tensor_copy(dst[:, 0, :], x[r][:].indirect(entries(own_list, h * HALF, (h + 1) * HALF)))
            nc.vector.tensor_copy(dst[:, 1, :], x[r][:].indirect(entries(partner_list, h * HALF, (h + 1) * HALF)))

        def subtract(grouped, pair, r):
            nc.gpsimd.tensor_tensor(grouped[:, :, r], pair[:, 0, :], pair[:, 1, :], ALU.subtract)

        def quantise(grouped, h, tag):
            codes = keep.tile([P, HALF], U32, name=f"d_codes{h}", tag=tag, align_bytes=64)
            scales = keep.tile([P, HALF], U8, name=f"d_scales{h}", align_bytes=64)
            nc.vector.quantize_mx(
                out=codes[:].bitcast(FP8X4), scales=scales[:], in_=grouped[:].rearrange("p c r -> p (c r)")
            )
            return codes, scales

        def multiply(codes, scales, h, urgent):
            banks = [psum.tile([P, HALF], F32, name=f"turned{h}{r}", tag=f"turned{r}") for r in range(PACK)]
            sums = []
            for b in range(2):
                cols = slice(b * P, (b + 1) * P)
                acc = psum.tile([P, N], F32, name=f"acc{h}{b}")
                nc.tensor.matmul_mx(
                    out=acc[:],
                    lhsT=codes[:, cols].bitcast(FP8X4),
                    lhsT_scale=scales[:, cols],
                    rhs=w_codes[:].bitcast(FP8X4),
                    rhs_scale=w_scales[:],
                    start=True,
                    stop=True,
                )
                sums.append(acc[:].rearrange("p (m r) -> p r m", r=PACK))
            for first, last in ((0, 1), (1, PACK)):
                for b in range(2):
                    gated = keep.tile(
                        [P, last - first, P], F32, name=f"gated{h}{b}{first}", tag=f"gated{h}{b}{first}"
                    )
                    nc.scalar.activation(
                        out=gated[:],
                        in_=sums[b][:, first:last, :],
                        func=COPY,
                        scale=gate[:, 2 * h + b : 2 * h + b + 1],
                    )
                    for r in range(first, last):
                        nc.tensor.transpose(banks[r][:, b * P : (b + 1) * P], gated[:, r - first, :], ident[:])
                if first == 0:
                    nc.scalar.copy(out=urgent, in_=banks[0][:, : urgent.shape[1]])
            return banks

        def scatter(r, a, b, values):
            nc.vector.tensor_copy(placed[r][:].indirect(entries(partner_list, a, b)), values)

        grouped0 = keep.tile([P, HALF, PACK], BF16, name="grouped0", tag="grouped", align_bytes=64)
        for r in range(PACK):
            pair = keep.tile([P, 2, HALF], F32, name=f"pair0{r}", tag=f"pair0{r}")
            gather_pair(pair, r, 0)
            subtract(grouped0, pair, r)
        pair13 = keep.tile([P, 2, HALF], F32, name="pair13")
        gather_pair(pair13, 3, 1)
        codes0, scales0 = quantise(grouped0, 0, "d_codes0")
        halved0 = keep.tile([P, T], F32, name="halved0")
        nc.scalar.activation(out=halved0[:], in_=old_sb[0][:], func=COPY, scale=0.5)
        pw_first = keep.tile([P, P], F32, name="pw_first", tag="pw_first", align_bytes=64)
        banks0 = multiply(codes0, scales0, 0, pw_first[:])
        pw_late = keep.tile([P, 2, J], F32, name="pw_late")
        for r in range(2, PACK):
            nc.scalar.copy(out=pw_late[:, r - 2, :HALF], in_=banks0[r][:])

        grouped1 = keep.tile([P, HALF, PACK], BF16, name="grouped1", tag="grouped", align_bytes=64)
        subtract(grouped1, pair13, 3)
        pairs1 = keep.tile([P, 3, 2, HALF], F32, name="pairs1", tag="pair03")
        for r in (2, 1, 0):
            gather_pair(pairs1[:, r, :, :], r, 1)
            subtract(grouped1, pairs1[:, r, :, :], r)
        scatter(0, 0, P, pw_first[:])
        codes1, scales1 = quantise(grouped1, 1, "pw_first")
        pw_next = keep.tile([P, P + HALF], F32, name="pw_next", tag="pair03")
        nc.scalar.copy(out=pw_next[:, :P], in_=banks0[0][:, P:])
        nc.scalar.copy(out=pw_next[:, P:], in_=banks0[1][:])
        scatter(0, P, HALF, pw_next[:, :P])
        scatter(1, 0, HALF, pw_next[:, P:])

        pw1 = keep.tile([P, 2, HALF], F32, name="pw1")
        banks1 = multiply(codes1, scales1, 1, pw1[:, 0, :])
        nc.scalar.copy(out=pw1[:, 1, :], in_=banks1[1][:])
        for r in range(2, PACK):
            nc.scalar.copy(out=pw_late[:, r - 2, HALF:], in_=banks1[r][:])

        halved1 = keep.tile([P, T], F32, name="halved1", tag="gated101")
        y = keep.tile([P, PACK, T], F32, name="y", tag="gated111")
        halved = [halved0[:], halved1[:], y[:, 3, :]]
        for r in range(1, 3):
            nc.scalar.activation(out=halved[r], in_=old_sb[r][:], func=COPY, scale=0.5)
        y_grouped = keep.tile([P, T, PACK], BF16, name="y_grouped", align_bytes=64)
        y_codes = keep.tile([P, T], U32, name="y_codes", align_bytes=64)
        y_scales = keep.tile([P, T], U8, name="y_scales", align_bytes=64)

        def pair_views(first, cols):
            dst = y_grouped[:, cols, first : first + 2].rearrange("p (c i) r -> p c r i", i=2)
            src = y[:, first : first + 2, cols].rearrange("p r (c i) -> p c r i", i=2)
            return dst, src

        def combine_gpsimd(r, cols):
            nc.gpsimd.tensor_tensor(y[:, r, cols], halved[r][:, cols], placed[r][:, cols], ALU.subtract)

        def combine_vector(r, cols):
            nc.vector.scalar_tensor_tensor(
                y[:, r, cols], old_sb[r][:, cols], 0.5, placed[r][:, cols], ALU.mult, ALU.subtract
            )

        left, right = slice(0, T // 2), slice(T // 2, T)
        chunks = [slice(c * CHUNK, (c + 1) * CHUNK) for c in range(T // CHUNK)]

        scatter(0, HALF, J, pw1[:, 0, :])
        combine_gpsimd(0, slice(0, T))
        nc.sync.dma_start(out=out_rows[:, 0, :], in_=y[:, 0, :])
        scatter(1, HALF, J, pw1[:, 1, :])
        for cols in (left, right):
            combine_gpsimd(1, cols)
            dst, src = pair_views(0, cols)
            nc.scalar.copy(out=dst, in_=src)
        nc.sync.dma_start(out=out_rows[:, 1, :], in_=y[:, 1, :])
        scatter(2, 0, J, pw_late[:, 0, :])
        for cols in (left, right):
            combine_gpsimd(2, cols)
            nc.sync.dma_start(out=out_rows[:, 2, cols], in_=y[:, 2, cols])
        scatter(3, 0, J, pw_late[:, 1, :])

        combine_vector(3, chunks[0])
        combine_vector(3, chunks[1])
        nc.sync.dma_start(out=out_rows[:, 3, left], in_=y[:, 3, left])
        combine_vector(3, chunks[2])
        combine_vector(3, chunks[3])
        nc.sync.dma_start(out=out_rows[:, 3, right], in_=y[:, 3, right])

        words_out = out_1[0].rearrange("p c r -> p (c r)").bitcast(I32)

        def quantise_y(cols):
            nc.vector.quantize_mx(
                out=y_codes[:, cols].bitcast(FP8X4),
                scales=y_scales[:, cols],
                in_=y_grouped[:, cols, :].rearrange("p c r -> p (c r)"),
            )

        def store_words(cols):
            nc.sync.dma_start(out=words_out[:, cols], in_=y_codes[:, cols].bitcast(I32))

        for cols in (chunks[0], chunks[1], slice(T - P, T)):
            dst, src = pair_views(2, cols)
            nc.scalar.copy(out=dst, in_=src)
        dst, src = pair_views(2, slice(T // 2, T - P))
        nc.vector.tensor_copy(out=dst, in_=src)
        quantise_y(chunks[0])
        quantise_y(chunks[1])
        store_words(left)
        quantise_y(right)
        store_words(right)
        for q in range(4):
            eng = nc.scalar if q % 2 == 0 else nc.sync
            eng.dma_start(
                out=out_2[0, 4 * q : 4 * q + 4, :].bitcast(I32),
                in_=y_scales[32 * q : 32 * q + 4, :].bitcast(I32),
            )
